import numpy as np
import ml_dtypes


def mxq(x, axis, fmt="e4m3"):
    dtype, down = {"e4m3": (ml_dtypes.float8_e4m3fn, 7), "e5m2": (ml_dtypes.float8_e5m2, 14)}[fmt]
    v = np.moveaxis(np.asarray(x, np.float32).astype(ml_dtypes.bfloat16).astype(np.float64), axis, -1)
    blocks = v.reshape(v.shape[:-1] + (-1, 32))
    amax = np.abs(blocks).max(-1, keepdims=True)
    byte = np.maximum(np.where(amax > 0, np.frexp(amax)[1] - 1 + 127, 0) - down, 1)
    scale = np.exp2(byte - 127.0)
    codes = (blocks / scale).astype(np.float32).astype(dtype).astype(np.float64)
    return np.moveaxis((codes * scale).reshape(v.shape), -1, axis)


WIDE = False


def mx_kscale(k):
    if not WIDE:
        return np.ones(k)
    levels = np.array([10, -10, 5, -5, 0])
    if k % 512:
        return np.exp2(np.random.permutation(np.resize(levels, k // 32))).repeat(32)
    a = np.empty((k // 512, 16))
    for p in range(k // 512):
        a[p, :8] = np.random.permutation(np.resize(levels, 8))
        for g in range(8):
            far = levels[np.abs(levels - a[p, g]) >= 10]
            a[p, g + 8] = far[np.random.randint(len(far))]
    return np.exp2(a.ravel()).repeat(32)


def f64(x):
    return np.asarray(x).astype(np.float64)


def striped(idx):
    return np.tile(idx.reshape(-1, 16).T, (8, 1)).astype(np.uint16)


def unstriped(offs):
    return offs[:16].T.reshape(-1).astype(np.int64)


E2M1 = np.array([0.0, 0.5, 1.0, 1.5, 2.0, 3.0, 4.0, 6.0, -0.0, -0.5, -1.0, -1.5, -2.0, -3.0, -4.0, -6.0])


def pack_weight(w, fmt):
    k, n = w.shape
    w = f64(np.asarray(w, np.float32).astype(ml_dtypes.bfloat16)).reshape(k // 32, 32, n)
    amax = np.abs(w).max(1)
    if fmt == "e4m3":
        byte = np.frexp(amax)[1] - 1 + 127 - 7
    else:
        mant, ex = np.frexp(amax / 6.0)
        byte = np.where(mant > 0.5, ex, ex - 1) + 127
    byte = np.clip(np.where(amax > 0, byte, 1), 1, 254)
    scaled = (w * np.exp2(127.0 - byte)[:, None, :]).reshape(k, n).astype(np.float32)
    by_word = np.ascontiguousarray(scaled.reshape(k // 512, 128, 4, n).transpose(0, 1, 3, 2))
    if fmt == "e4m3":
        words = by_word.astype(ml_dtypes.float8_e4m3fn).view(np.uint8)
    else:
        c = by_word.astype(ml_dtypes.float4_e2m1fn).view(np.uint8) & 0xF
        words = (c[..., 0::2] | (c[..., 1::2] << 4)).reshape(k // 512, 128, 2 * n)
    return np.ascontiguousarray(words), np.ascontiguousarray(byte.astype(np.uint8).reshape(k // 512, 16, n))


def unpack_weight(words, scales, fmt):
    g, _, n = scales.shape
    words = np.ascontiguousarray(words).reshape(g, 128, n, -1)
    if fmt == "e4m3":
        vals = words.view(ml_dtypes.float8_e4m3fn).astype(np.float64)
    else:
        nib = np.empty((g, 128, n, 4), np.uint8)
        nib[..., 0::2] = words & 0xF
        nib[..., 1::2] = words >> 4
        vals = E2M1[nib]
    vals = vals * np.repeat(np.exp2(scales.astype(np.float64) - 127.0), 8, axis=1)[..., None]
    return vals.transpose(0, 1, 3, 2).reshape(g * 512, n)


def gelu(v):
    return 0.5 * v * (1.0 + np.tanh(np.sqrt(2.0 / np.pi) * (v + 0.044715 * v**3)))


K, H, N, T, S, P = 512, 1024, 384, 2048, 1024, 512


def setup_inputs():
    n = np.random.standard_normal
    s = mx_kscale(K)[:, None]
    u = mx_kscale(H)[:, None]
    tab_words, tab_scales = pack_weight(n((K, T)) * s, "e4m3")
    w2_words, w2_scales = pack_weight(0.97 * n((K, H)) / np.sqrt(K) / s, "e2m1")
    w4_words, w4_scales = pack_weight(n((H, N)) / np.sqrt(H) / u, "e4m3")
    return {
        "tab_words": tab_words, "tab_scales": tab_scales,
        "offs": striped(np.random.permutation(T)[:S]),
        "pos1": striped(np.random.permutation(S)[:P]),
        "pos2": striped(np.random.permutation(S)[:P]),
        "w1": (0.72 * n((K, H)) / np.sqrt(K) / s).astype(np.float32),
        "w2_words": w2_words, "w2_scales": w2_scales,
        "temp": np.random.uniform(0.4, 1.6, H).astype(np.float32),
        "shift": (0.5 * n(H)).astype(np.float32),
        "thr": n(H).astype(np.float32),
        "lift": (0.35 * n(H)).astype(np.float32),
        "mat": (0.6 * n((H, P)) * u).astype(np.float32),
        "w3": (1.3 * n((H, H)) / np.sqrt(H) / u).astype(np.float32),
        "gain": (np.random.uniform(0.6, 1.8, H) * u[:, 0]).astype(np.float32),
        "w4_words": w4_words, "w4_scales": w4_scales,
    }


def reference(tab_words, tab_scales, offs, pos1, pos2, w1, w2_words, w2_scales, temp, shift, thr, lift, mat, w3, gain, w4_words, w4_scales):
    v = unpack_weight(tab_words, tab_scales, "e4m3")[:, unstriped(offs)]
    w1q = mxq(f64(w1), 0, "e4m3")
    w2 = unpack_weight(w2_words, w2_scales, "e2m1")
    h = w1q.T @ v
    g = w2.T @ v
    a = np.exp(f64(temp)[:, None] * h[:, unstriped(pos1)] + f64(shift)[:, None])
    c = 1.0 / (1.0 + np.exp(-(g[:, unstriped(pos2)] + f64(thr)[:, None])))
    z = (c + f64(lift)[:, None]) * a * f64(mat)
    zq = mxq(z, 0, "e4m3")
    w3q = mxq(f64(w3), 0, "e4m3")
    y = z + f64(gain)[:, None] * np.tanh(w3q.T @ zq)
    yq = mxq(y, 0, "e4m3")
    w4 = unpack_weight(w4_words, w4_scales, "e4m3")
    out = w4.T @ yq
    return out

@@ -1,0 +1,277 @@
+from contextlib import ExitStack
+
+import concourse.mybir as mybir
+
+K, H, N, T, S, PAIRS = 512, 1024, 384, 2048, 1024, 512
+FLOPS = 2 * (2 * K * H * S + H * H * PAIRS + H * N * PAIRS)
+
+F32 = mybir.dt.float32
+BF16 = mybir.dt.bfloat16
+I32 = mybir.dt.int32
+U32 = mybir.dt.uint32
+U16 = mybir.dt.uint16
+U8 = mybir.dt.uint8
+FP8X4 = mybir.dt.float8_e4m3fn_x4
+FP4X4 = mybir.dt.float4_e2m1fn_x4
+ACT = mybir.ActivationFunctionType
+ALU = mybir.AluOpType
+
+P = 128
+PACK = 4
+K_PASS = P * PACK
+BANK = 512
+ROW_PASSES = H // K_PASS
+ROW_TILES = H // P
+HALF = PAIRS // 2
+G_BANKS_ON_SCALAR = 3
+W1_ROUND_AFTER = (2, 5)
+H_BANKS_ON_VECTOR = 4
+
+
+def tile_list_suction_seal_scores_kernel(
+    tc, tab_words, tab_scales, offs, pos1, pos2, w1, w2_words, w2_scales,
+    temp, shift, thr, lift, mat, w3, gain, w4_words, w4_scales, out,
+):
+    nc = tc.nc
+    with ExitStack() as ctx:
+        lists = ctx.enter_context(tc.tile_pool(name="lists", bufs=1))
+        keep = ctx.enter_context(tc.tile_pool(name="keep", bufs=1))
+        work = ctx.enter_context(tc.tile_pool(name="work", bufs=1))
+        psum = ctx.enter_context(tc.psum_pool(name="psum", bufs=8))
+
+        def load_scale_rows(queues, plane, rows):
+            for q, queue in enumerate(queues):
+                queue.dma_start(out=plane[32 * q : 32 * q + 4].bitcast(I32), in_=rows[4 * q : 4 * q + 4].bitcast(I32))
+
+        def load_row_vector(queue, vec, name):
+            tile = keep.tile([P, ROW_TILES], F32, name=name)
+            queue.dma_start(
+                out=tile[:].rearrange("p (b t) -> p b t", t=PACK),
+                in_=vec.rearrange("(b p t) -> p b t", p=P, t=PACK),
+            )
+            return tile
+
+        tab_s = work.tile([P, T], U8, tag="picked", bufs=1, align_bytes=64)
+        w2_s_raw = keep.tile([P, H], U8, align_bytes=64)
+        w4_s = keep.tile([P, ROW_PASSES, N], U8, align_bytes=64)
+        nc.gpsimd.memset(tab_s[:].bitcast(I32), 0)
+        nc.vector.memset(w2_s_raw[:].bitcast(I32), 0)
+
+        offs_sb = lists.tile([P, S // 16], U16)
+        nc.sync.dma_start(offs_sb[:], offs)
+        load_scale_rows([nc.scalar] * 4, tab_s, tab_scales[0])
+        tab_w = keep.tile([P, T], U32, align_bytes=64)
+        nc.sync.dma_start(out=tab_w[:].bitcast(I32), in_=tab_words[0].rearrange("p t i -> p (t i)").bitcast(I32))
+        w2_w_raw = keep.tile([P, 2 * H], U8, align_bytes=64)
+        nc.sync.dma_start(out=w2_w_raw[:].bitcast(I32), in_=w2_words[0].bitcast(I32))
+        load_scale_rows([nc.gpsimd, nc.gpsimd, nc.sync, nc.sync], w2_s_raw, w2_scales[0])
+        nc.vector.memset(w4_s[:].rearrange("p a n -> p (a n)").bitcast(I32), 0)
+
+        def load_weight_block(w, a, b, name):
+            raw = keep.tile([P, PACK, K_PASS], F32, name=name)
+            rows = w[a * K_PASS : (a + 1) * K_PASS, b * K_PASS : (b + 1) * K_PASS]
+            nc.sync.dma_start(out=raw[:], in_=rows.rearrange("(p j) c -> p j c", j=PACK))
+            return raw
+
+        def load_mat():
+            tiles = []
+            for b in range(ROW_PASSES):
+                tile = keep.tile([P, PACK, PAIRS], F32, name=f"mat_sb{b}")
+                nc.sync.dma_start(out=tile[:], in_=mat[b * K_PASS : (b + 1) * K_PASS].rearrange("(p t) c -> p t c", t=PACK))
+                tiles.append(tile)
+            return tiles
+
+        w1_raw = [load_weight_block(w1, 0, 0, "w1_raw0")]
+        pos2_sb = lists.tile([P, PAIRS // 16], U16)
+        nc.sync.dma_start(pos2_sb[:], pos2)
+        thr_sb = load_row_vector(nc.sync, thr, "thr_sb")
+        w1_raw.append(load_weight_block(w1, 0, 1, "w1_raw1"))
+        pos1_sb = lists.tile([P, PAIRS // 16], U16)
+        nc.sync.dma_start(pos1_sb[:], pos1)
+        temp_sb = load_row_vector(nc.sync, temp, "temp_sb")
+        shift_sb = load_row_vector(nc.sync, shift, "shift_sb")
+        lift_sb = load_row_vector(nc.sync, lift, "lift_sb")
+        z = load_mat()
+        gain_sb = load_row_vector(nc.sync, gain, "gain_sb")
+        w3_raw = {(a, b): load_weight_block(w3, a, b, f"w3_raw{a}{b}") for b in range(ROW_PASSES) for a in range(ROW_PASSES)}
+        w4_w = keep.tile([P, ROW_PASSES, N], U32, align_bytes=64)
+        nc.sync.dma_start(out=w4_w[:].bitcast(I32), in_=w4_words.rearrange("a p n i -> p a (n i)").bitcast(I32))
+        load_scale_rows([nc.sync] * 4, w4_s, w4_scales.rearrange("a r n -> r a n"))
+
+        v_w, v_s = [], []
+        for c in range(S // BANK):
+            picked = keep.tile([P, BANK], U8, name=f"v_s{c}", align_bytes=64)
+            nc.vector.tensor_copy(picked[:], tab_s[:].indirect(offs_sb[:, 32 * c : 32 * (c + 1)]))
+            v_s.append(picked)
+        picked_words = work.tile([P, S], U32, tag="picked", bufs=1, align_bytes=64)
+        for c in range(S // BANK):
+            picked = picked_words[:, c * BANK : (c + 1) * BANK]
+            nc.vector.tensor_copy(picked, tab_w[:].indirect(offs_sb[:, 32 * c : 32 * (c + 1)]))
+            v_w.append(picked)
+
+        w2_w, w2_s = [], []
+        for b in range(ROW_PASSES):
+            words = keep.tile([P, 2 * K_PASS], U8, name=f"w2_w{b}", align_bytes=64)
+            nc.scalar.copy(
+                out=words[:].bitcast(U16).rearrange("p (t m) -> p t m", t=PACK),
+                in_=w2_w_raw[:, 2 * K_PASS * b : 2 * K_PASS * (b + 1)].bitcast(U16).rearrange("p (m t) -> p t m", t=PACK),
+            )
+            scales = keep.tile([P, K_PASS], U8, name=f"w2_s{b}", align_bytes=64)
+            for t in range(PACK):
+                nc.gpsimd.tensor_copy(
+                    out=scales[:, P * t : P * (t + 1)],
+                    in_=w2_s_raw[:, K_PASS * b + t : K_PASS * (b + 1) : PACK],
+                )
+            w2_w.append(words)
+            w2_s.append(scales)
+
+        def quantize(grouped, name):
+            width = grouped.shape[1] // PACK
+            codes = keep.tile([P, width], U32, name=name + "_w", align_bytes=64)
+            scales = keep.tile([P, width], U8, name=name + "_s", align_bytes=64)
+            nc.vector.quantize_mx(out=codes[:].bitcast(FP8X4), scales=scales[:], in_=grouped[:])
+            return codes, scales
+
+        def round_weight_block(raw, on_gpsimd):
+            grouped = work.tile([P, PACK * K_PASS], BF16, tag="wbf", bufs=3, align_bytes=64)
+            dst = grouped[:].rearrange("p (u e m j) -> p u m j e", u=2, e=2, j=PACK)
+            src = raw[:].rearrange("p j (m u e) -> p u m j e", u=2, e=2)
+            if on_gpsimd:
+                for u in range(2):
+                    nc.gpsimd.tensor_scalar(dst[:, u], src[:, u], 1.0, 0.0, ALU.mult, ALU.add)
+            else:
+                nc.vector.tensor_copy(out=dst, in_=src)
+            return grouped
+
+        def first_stage(lhs_w, lhs_s, rows, chunks, on_scalar):
+            for c in chunks:
+                bank = psum.tile([P, BANK], F32, tag="bank")
+                nc.tensor.matmul_mx(out=bank[:], lhsT=lhs_w, lhsT_scale=lhs_s, rhs=v_w[c][:].bitcast(FP8X4), rhs_scale=v_s[c][:], start=True, stop=True)
+                if on_scalar(c):
+                    nc.scalar.copy(out=rows[:, c * BANK : (c + 1) * BANK], in_=bank[:])
+                else:
+                    nc.vector.tensor_copy(out=rows[:, c * BANK : (c + 1) * BANK], in_=bank[:])
+
+        def gate_curved(curved, k):
+            b, t = divmod(k, PACK)
+            nc.vector.scalar_tensor_tensor(z[b][:, t, :], curved[:], lift_sb[:, k : k + 1], z[b][:, t, :], ALU.add, ALU.mult)
+
+        def interleave(planes, on_scalar=False):
+            grouped = work.tile([P, PACK * HALF], BF16, tag="abf", bufs=4, align_bytes=64)
+            copy = nc.scalar.copy if on_scalar else nc.vector.tensor_copy
+            copy(
+                out=grouped[:].rearrange("p (c i t) -> p c t i", i=4, t=PACK),
+                in_=planes.rearrange("p t (c i) -> p c t i", i=4),
+            )
+            return grouped
+
+        w1_q = []
+        curved = []
+        for k in range(ROW_TILES):
+            b, t = divmod(k, PACK)
+            last = k >= ROW_TILES - 2
+            g = work.tile([P, S], F32, tag=f"turn{ROW_TILES - 1 - k}" if last else "rows", bufs=1 if last else 8)
+            first_stage(
+                w2_w[b][:, 2 * P * t : 2 * P * (t + 1)].bitcast(FP4X4), w2_s[b][:, P * t : P * (t + 1)], g, (0, 1),
+                lambda c: c == 0 and k < G_BANKS_ON_SCALAR,
+            )
+            tile = work.tile([P, PAIRS], F32, tag="curved", bufs=8)
+            nc.scalar.activation(out=tile[:], in_=g[:].indirect(pos2_sb[:]), func=ACT.Sigmoid, bias=thr_sb[:, k : k + 1])
+            curved.append(tile)
+            if k in W1_ROUND_AFTER:
+                w1_bf = round_weight_block(w1_raw[len(w1_q)], False)
+            if k - 1 in W1_ROUND_AFTER:
+                w1_q.append(quantize(w1_bf, f"w1_q{len(w1_q)}"))
+
+        flat = {}
+
+        def look_flat(h, k, half):
+            b, t = divmod(k, PACK)
+            if t == 0:
+                first = b == 0
+                flat[b, half] = work.tile([P, PACK, HALF], F32, name="flat", tag=f"turn{half}" if first else "flat", bufs=1 if first else 2)
+            nc.scalar.activation(
+                out=flat[b, half][:, t, :], in_=h[:].indirect(pos1_sb[:, 16 * half : 16 * (half + 1)]), func=ACT.Exp,
+                bias=shift_sb[:, k : k + 1], scale=temp_sb[:, k : k + 1],
+            )
+
+        def finish_z(b, half, ts):
+            cols = slice(half * HALF, (half + 1) * HALF)
+            nc.vector.tensor_tensor(z[b][:, ts, cols], z[b][:, ts, cols], flat[b, half][:, ts, :], ALU.mult)
+
+        def h_stage(k, chunks, on_scalar):
+            b, t = divmod(k, PACK)
+            codes, scales = w1_q[b]
+            first_stage(codes[:, P * t : P * (t + 1)].bitcast(FP8X4), scales[:, P * t : P * (t + 1)], h_rows[k], chunks, lambda c: on_scalar)
+
+        h_rows = []
+        w3_q = {}
+        z_q = {}
+        for k in range(ROW_TILES):
+            h = work.tile([P, S], F32, tag="rows", bufs=8)
+            h_rows.append(h)
+            for c in range(S // BANK):
+                h_stage(k, (c,), 2 * k + c >= H_BANKS_ON_VECTOR)
+            look_flat(h, k, 0)
+            if k < PACK:
+                look_flat(h, k, 1)
+        for k in range(PACK, ROW_TILES):
+            look_flat(h_rows[k], k, 1)
+
+        def finish_and_quantize_z(b, half):
+            for u in range(4):
+                finish_z(b, half, slice(u * 1, (u + 1) * 1))
+            z_q[b, half] = quantize(interleave(z[b][:, :, half * HALF : (half + 1) * HALF]), f"z_q{b}{half}")
+
+        w3_order = list(w3_raw)
+        for step in range(len(w3_order)):
+            gate_curved(curved[2 * step], 2 * step)
+            rounded = round_weight_block(w3_raw[w3_order[step]], False)
+            gate_curved(curved[2 * step + 1], 2 * step + 1)
+            w3_q[w3_order[step]] = quantize(rounded, f"w3_q{step}")
+        for b in range(ROW_PASSES):
+            for half in range(2):
+                finish_and_quantize_z(b, half)
+
+        y = {}
+        for half in range(2):
+            for b in range(ROW_PASSES):
+                y[b, half] = work.tile([P, PACK, HALF], F32, name="y", tag="y", bufs=4)
+                for u in range(2):
+                    bank = psum.tile([P, 2, HALF], F32, tag="bank")
+                    for e in range(2):
+                        t = 2 * u + e
+                        for a in range(ROW_PASSES):
+                            codes, scales = w3_q[a, b]
+                            nc.tensor.matmul_mx(
+                                out=bank[:, e, :], lhsT=codes[:, P * t : P * (t + 1)].bitcast(FP8X4), lhsT_scale=scales[:, P * t : P * (t + 1)],
+                                rhs=z_q[a, half][0][:].bitcast(FP8X4), rhs_scale=z_q[a, half][1][:],
+                                start=(a == 0), stop=(a == ROW_PASSES - 1),
+                            )
+                    nc.scalar.activation(out=y[b, half][:, 2 * u : 2 * u + 2, :], in_=bank[:], func=ACT.Tanh)
+
+        out_rows = out.rearrange("(n p) j -> p n j", p=P)
+        for half in range(2):
+            cols = slice(half * HALF, (half + 1) * HALF)
+            y_q = []
+            for b in range(ROW_PASSES):
+                for t in range(PACK):
+                    k = PACK * b + t
+                    plane = y[b, half][:, t, :]
+                    nc.vector.scalar_tensor_tensor(plane, plane, gain_sb[:, k : k + 1], z[b][:, t, cols], ALU.mult, ALU.add)
+                y_q.append(quantize(interleave(y[b, half][:], 2 * half + b < 2), f"y_q{b}{half}"))
+            scores = work.tile([P, N // P, HALF], F32, tag="scores", bufs=2)
+            for n in range(N // P):
+                bank = psum.tile([P, HALF], F32, tag="bank")
+                n_cols = slice(P * n, P * (n + 1))
+                for a in range(ROW_PASSES):
+                    nc.tensor.matmul_mx(
+                        out=bank[:], lhsT=w4_w[:, a, n_cols].bitcast(FP8X4), lhsT_scale=w4_s[:, a, n_cols],
+                        rhs=y_q[a][0][:].bitcast(FP8X4), rhs_scale=y_q[a][1][:],
+                        start=(a == 0), stop=(a == ROW_PASSES - 1),
+                    )
+                if half == 1 and n == 1:
+                    nc.vector.tensor_copy(out=scores[:, n, :], in_=bank[:])
+                else:
+                    nc.scalar.copy(out=scores[:, n, :], in_=bank[:])
+            nc.sync.dma_start(out=out_rows[:, :, cols], in_=scores[:])

@@ -23,7 +23,7 @@ BANK = 512
 ROW_PASSES = H // K_PASS
 ROW_TILES = H // P
 HALF = PAIRS // 2
-G_BANKS_ON_SCALAR = 3
+G_BANKS_ON_SCALAR = 4
 W1_ROUND_AFTER = (2, 5)
 H_BANKS_ON_VECTOR = 4
 
@@ -117,11 +117,10 @@ def tile_list_suction_seal_scores_kernel(
                 in_=w2_w_raw[:, 2 * K_PASS * b : 2 * K_PASS * (b + 1)].bitcast(U16).rearrange("p (m t) -> p t m", t=PACK),
             )
             scales = keep.tile([P, K_PASS], U8, name=f"w2_s{b}", align_bytes=64)
-            for t in range(PACK):
-                nc.gpsimd.tensor_copy(
-                    out=scales[:, P * t : P * (t + 1)],
-                    in_=w2_s_raw[:, K_PASS * b + t : K_PASS * (b + 1) : PACK],
-                )
+            nc.vector.tensor_copy(
+                out=scales[:].rearrange("p (t m) -> p t m", t=PACK),
+                in_=w2_s_raw[:, K_PASS * b : K_PASS * (b + 1)].rearrange("p (m t) -> p t m", t=PACK),
+            )
             w2_w.append(words)
             w2_s.append(scales)
 
@@ -165,18 +164,26 @@ def tile_list_suction_seal_scores_kernel(
             )
             return grouped
 
+        def g_stage(k, c, on_scalar):
+            b, t = divmod(k, PACK)
+            first_stage(w2_w[b][:, 2 * P * t : 2 * P * (t + 1)].bitcast(FP4X4), w2_s[b][:, P * t : P * (t + 1)], g_rows[k], (c,), lambda c: on_scalar)
+
         w1_q = []
         curved = []
+        g_rows = []
+        for k in range(G_BANKS_ON_SCALAR):
+            g = work.tile([P, S], F32, tag="rows", bufs=8)
+            g_rows.append(g)
+            g_stage(k, 0, True)
         for k in range(ROW_TILES):
-            b, t = divmod(k, PACK)
             last = k >= ROW_TILES - 2
-            g = work.tile([P, S], F32, tag=f"turn{ROW_TILES - 1 - k}" if last else "rows", bufs=1 if last else 8)
-            first_stage(
-                w2_w[b][:, 2 * P * t : 2 * P * (t + 1)].bitcast(FP4X4), w2_s[b][:, P * t : P * (t + 1)], g, (0, 1),
-                lambda c: c == 0 and k < G_BANKS_ON_SCALAR,
-            )
+            if k >= G_BANKS_ON_SCALAR:
+                g = work.tile([P, S], F32, tag=f"turn{ROW_TILES - 1 - k}" if last else "rows", bufs=1 if last else 8)
+                g_rows.append(g)
+                g_stage(k, 0, False)
+            g_stage(k, 1, False)
             tile = work.tile([P, PAIRS], F32, tag="curved", bufs=8)
-            nc.scalar.activation(out=tile[:], in_=g[:].indirect(pos2_sb[:]), func=ACT.Sigmoid, bias=thr_sb[:, k : k + 1])
+            nc.scalar.activation(out=tile[:], in_=g_rows[k][:].indirect(pos2_sb[:]), func=ACT.Sigmoid, bias=thr_sb[:, k : k + 1])
             curved.append(tile)
             if k in W1_ROUND_AFTER:
                 w1_bf = round_weight_block(w1_raw[len(w1_q)], False)
@@ -239,14 +246,14 @@ def tile_list_suction_seal_scores_kernel(
                 y[b, half] = work.tile([P, PACK, HALF], F32, name="y", tag="y", bufs=4)
                 for u in range(2):
                     bank = psum.tile([P, 2, HALF], F32, tag="bank")
-                    for e in range(2):
-                        t = 2 * u + e
-                        for a in range(ROW_PASSES):
+                    for a in range(ROW_PASSES):
+                        for e in range(2):
+                            t = 2 * u + e
                             codes, scales = w3_q[a, b]
                             nc.tensor.matmul_mx(
                                 out=bank[:, e, :], lhsT=codes[:, P * t : P * (t + 1)].bitcast(FP8X4), lhsT_scale=scales[:, P * t : P * (t + 1)],
                                 rhs=z_q[a, half][0][:].bitcast(FP8X4), rhs_scale=z_q[a, half][1][:],
-                                start=(a == 0), stop=(a == ROW_PASSES - 1),
+                                start=(a == 0 and e == 0), stop=(a == ROW_PASSES - 1 and e == 1),
                             )
                     nc.scalar.activation(out=y[b, half][:, 2 * u : 2 * u + 2, :], in_=bank[:], func=ACT.Tanh)
 

@@ -19,13 +19,19 @@ ALU = mybir.AluOpType
 P = 128
 PACK = 4
 K_PASS = P * PACK
-BANK = 512
+CHUNK = 512
+CHUNKS = S // CHUNK
+PER_COLUMN = 16
 ROW_PASSES = H // K_PASS
 ROW_TILES = H // P
-HALF = PAIRS // 2
-G_BANKS_ON_SCALAR = 4
+HALVES = 2
+HALF = PAIRS // HALVES
+PSUM_BANKS = 8
+MX_ALIGN = 64
+
+G_BANKS_ON_SCALAR = 5
+H_BANKS_ON_VECTOR = 5
 W1_ROUND_AFTER = (2, 5)
-H_BANKS_ON_VECTOR = 4
 
 
 def tile_list_suction_seal_scores_kernel(
@@ -37,248 +43,250 @@ def tile_list_suction_seal_scores_kernel(
         lists = ctx.enter_context(tc.tile_pool(name="lists", bufs=1))
         keep = ctx.enter_context(tc.tile_pool(name="keep", bufs=1))
         work = ctx.enter_context(tc.tile_pool(name="work", bufs=1))
-        psum = ctx.enter_context(tc.psum_pool(name="psum", bufs=8))
+        psum = ctx.enter_context(tc.psum_pool(name="psum", bufs=PSUM_BANKS))
 
-        def load_scale_rows(queues, plane, rows):
-            for q, queue in enumerate(queues):
-                queue.dma_start(out=plane[32 * q : 32 * q + 4].bitcast(I32), in_=rows[4 * q : 4 * q + 4].bitcast(I32))
 
-        def load_row_vector(queue, vec, name):
-            tile = keep.tile([P, ROW_TILES], F32, name=name)
-            queue.dma_start(
-                out=tile[:].rearrange("p (b t) -> p b t", t=PACK),
+        def load_scale_rows(queue, scale_tile, rows):
+            for quadrant in range(4):
+                queue.dma_start(
+                    out=scale_tile[32 * quadrant : 32 * quadrant + 4].bitcast(I32),
+                    in_=rows[4 * quadrant : 4 * quadrant + 4].bitcast(I32),
+                )
+
+        def load_row_vector(vec, name):
+            columns = keep.tile([P, ROW_TILES], F32, name=name)
+            nc.sync.dma_start(
+                out=columns[:].rearrange("p (b t) -> p b t", t=PACK),
                 in_=vec.rearrange("(b p t) -> p b t", p=P, t=PACK),
             )
-            return tile
+            return columns
 
-        tab_s = work.tile([P, T], U8, tag="picked", bufs=1, align_bytes=64)
-        w2_s_raw = keep.tile([P, H], U8, align_bytes=64)
-        w4_s = keep.tile([P, ROW_PASSES, N], U8, align_bytes=64)
-        nc.gpsimd.memset(tab_s[:].bitcast(I32), 0)
-        nc.vector.memset(w2_s_raw[:].bitcast(I32), 0)
-
-        offs_sb = lists.tile([P, S // 16], U16)
-        nc.sync.dma_start(offs_sb[:], offs)
-        load_scale_rows([nc.scalar] * 4, tab_s, tab_scales[0])
-        tab_w = keep.tile([P, T], U32, align_bytes=64)
-        nc.sync.dma_start(out=tab_w[:].bitcast(I32), in_=tab_words[0].rearrange("p t i -> p (t i)").bitcast(I32))
-        w2_w_raw = keep.tile([P, 2 * H], U8, align_bytes=64)
-        nc.sync.dma_start(out=w2_w_raw[:].bitcast(I32), in_=w2_words[0].bitcast(I32))
-        load_scale_rows([nc.gpsimd, nc.gpsimd, nc.sync, nc.sync], w2_s_raw, w2_scales[0])
-        nc.vector.memset(w4_s[:].rearrange("p a n -> p (a n)").bitcast(I32), 0)
-
-        def load_weight_block(w, a, b, name):
+        def load_weight_group(w, a, b, name):
             raw = keep.tile([P, PACK, K_PASS], F32, name=name)
             rows = w[a * K_PASS : (a + 1) * K_PASS, b * K_PASS : (b + 1) * K_PASS]
             nc.sync.dma_start(out=raw[:], in_=rows.rearrange("(p j) c -> p j c", j=PACK))
             return raw
 
-        def load_mat():
-            tiles = []
-            for b in range(ROW_PASSES):
-                tile = keep.tile([P, PACK, PAIRS], F32, name=f"mat_sb{b}")
-                nc.sync.dma_start(out=tile[:], in_=mat[b * K_PASS : (b + 1) * K_PASS].rearrange("(p t) c -> p t c", t=PACK))
-                tiles.append(tile)
-            return tiles
+        tab_s = work.tile([P, T], U8, tag="tab_s_then_words", bufs=1, align_bytes=MX_ALIGN)
+        w2_s_raw = keep.tile([P, H], U8, align_bytes=MX_ALIGN)
+        w4_s = keep.tile([P, ROW_PASSES, N], U8, align_bytes=MX_ALIGN)
+        nc.gpsimd.memset(tab_s[:].bitcast(I32), 0)
+        nc.vector.memset(w2_s_raw[:].bitcast(I32), 0)
 
-        w1_raw = [load_weight_block(w1, 0, 0, "w1_raw0")]
-        pos2_sb = lists.tile([P, PAIRS // 16], U16)
+        offs_sb = lists.tile([P, S // PER_COLUMN], U16)
+        nc.sync.dma_start(offs_sb[:], offs)
+        load_scale_rows(nc.scalar, tab_s, tab_scales[0])
+        tab_w = keep.tile([P, T], U32, align_bytes=MX_ALIGN)
+        nc.sync.dma_start(out=tab_w[:].bitcast(I32), in_=tab_words[0].rearrange("p t i -> p (t i)").bitcast(I32))
+        w2_w_raw = keep.tile([P, 2 * H], U8, align_bytes=MX_ALIGN)
+        nc.sync.dma_start(out=w2_w_raw[:].bitcast(I32), in_=w2_words[0].bitcast(I32))
+        load_scale_rows(nc.sync, w2_s_raw, w2_scales[0])
+        nc.vector.memset(w4_s[:].rearrange("p a n -> p (a n)").bitcast(I32), 0)
+
+        w1_raw = [load_weight_group(w1, 0, 0, "w1_raw0")]
+        pos2_sb = lists.tile([P, PAIRS // PER_COLUMN], U16)
         nc.sync.dma_start(pos2_sb[:], pos2)
-        thr_sb = load_row_vector(nc.sync, thr, "thr_sb")
-        w1_raw.append(load_weight_block(w1, 0, 1, "w1_raw1"))
-        pos1_sb = lists.tile([P, PAIRS // 16], U16)
+        thr_sb = load_row_vector(thr, "thr_sb")
+        w1_raw.append(load_weight_group(w1, 0, 1, "w1_raw1"))
+        pos1_sb = lists.tile([P, PAIRS // PER_COLUMN], U16)
         nc.sync.dma_start(pos1_sb[:], pos1)
-        temp_sb = load_row_vector(nc.sync, temp, "temp_sb")
-        shift_sb = load_row_vector(nc.sync, shift, "shift_sb")
-        lift_sb = load_row_vector(nc.sync, lift, "lift_sb")
-        z = load_mat()
-        gain_sb = load_row_vector(nc.sync, gain, "gain_sb")
-        w3_raw = {(a, b): load_weight_block(w3, a, b, f"w3_raw{a}{b}") for b in range(ROW_PASSES) for a in range(ROW_PASSES)}
-        w4_w = keep.tile([P, ROW_PASSES, N], U32, align_bytes=64)
+        temp_sb = load_row_vector(temp, "temp_sb")
+        shift_sb = load_row_vector(shift, "shift_sb")
+        lift_sb = load_row_vector(lift, "lift_sb")
+        z = []
+        for b in range(ROW_PASSES):
+            mat_sb = keep.tile([P, PACK, PAIRS], F32, name=f"z{b}")
+            nc.sync.dma_start(out=mat_sb[:], in_=mat[b * K_PASS : (b + 1) * K_PASS].rearrange("(p t) c -> p t c", t=PACK))
+            z.append(mat_sb)
+        gain_sb = load_row_vector(gain, "gain_sb")
+        w3_raw = {
+            (a, b): load_weight_group(w3, a, b, f"w3_raw{a}{b}") for b in range(ROW_PASSES) for a in range(ROW_PASSES)
+        }
+        w4_w = keep.tile([P, ROW_PASSES, N], U32, align_bytes=MX_ALIGN)
         nc.sync.dma_start(out=w4_w[:].bitcast(I32), in_=w4_words.rearrange("a p n i -> p a (n i)").bitcast(I32))
-        load_scale_rows([nc.sync] * 4, w4_s, w4_scales.rearrange("a r n -> r a n"))
+        load_scale_rows(nc.sync, w4_s, w4_scales.rearrange("a r n -> r a n"))
 
+
+        chunk_offsets = [offs_sb[:, c * CHUNK // PER_COLUMN : (c + 1) * CHUNK // PER_COLUMN] for c in range(CHUNKS)]
         v_w, v_s = [], []
-        for c in range(S // BANK):
-            picked = keep.tile([P, BANK], U8, name=f"v_s{c}", align_bytes=64)
-            nc.vector.tensor_copy(picked[:], tab_s[:].indirect(offs_sb[:, 32 * c : 32 * (c + 1)]))
-            v_s.append(picked)
-        picked_words = work.tile([P, S], U32, tag="picked", bufs=1, align_bytes=64)
-        for c in range(S // BANK):
-            picked = picked_words[:, c * BANK : (c + 1) * BANK]
-            nc.vector.tensor_copy(picked, tab_w[:].indirect(offs_sb[:, 32 * c : 32 * (c + 1)]))
-            v_w.append(picked)
+        for c in range(CHUNKS):
+            picked_s = keep.tile([P, CHUNK], U8, name=f"v_s{c}", align_bytes=MX_ALIGN)
+            nc.vector.tensor_copy(picked_s[:], tab_s[:].indirect(chunk_offsets[c]))
+            v_s.append(picked_s)
+        for c in range(CHUNKS):
+            picked_w = work.tile([P, CHUNK], U32, tag="tab_s_then_words" if c else "v_w0", bufs=1, align_bytes=MX_ALIGN)
+            nc.vector.tensor_copy(picked_w[:], tab_w[:].indirect(chunk_offsets[c]))
+            v_w.append(picked_w)
+
 
         w2_w, w2_s = [], []
         for b in range(ROW_PASSES):
-            words = keep.tile([P, 2 * K_PASS], U8, name=f"w2_w{b}", align_bytes=64)
+            dealt_w = keep.tile([P, 2 * K_PASS], U8, name=f"w2_w{b}", align_bytes=MX_ALIGN)
             nc.scalar.copy(
-                out=words[:].bitcast(U16).rearrange("p (t m) -> p t m", t=PACK),
+                out=dealt_w[:].bitcast(U16).rearrange("p (t m) -> p t m", t=PACK),
                 in_=w2_w_raw[:, 2 * K_PASS * b : 2 * K_PASS * (b + 1)].bitcast(U16).rearrange("p (m t) -> p t m", t=PACK),
             )
-            scales = keep.tile([P, K_PASS], U8, name=f"w2_s{b}", align_bytes=64)
-            nc.vector.tensor_copy(
-                out=scales[:].rearrange("p (t m) -> p t m", t=PACK),
-                in_=w2_s_raw[:, K_PASS * b : K_PASS * (b + 1)].rearrange("p (m t) -> p t m", t=PACK),
-            )
-            w2_w.append(words)
-            w2_s.append(scales)
+            dealt_s = keep.tile([P, K_PASS], U8, name=f"w2_s{b}", align_bytes=MX_ALIGN)
+            for t in range(PACK):
+                nc.gpsimd.tensor_copy(
+                    out=dealt_s[:, P * t : P * (t + 1)],
+                    in_=w2_s_raw[:, K_PASS * b + t : K_PASS * (b + 1) : PACK],
+                )
+            w2_w.append(dealt_w)
+            w2_s.append(dealt_s)
+
 
         def quantize(grouped, name):
             width = grouped.shape[1] // PACK
-            codes = keep.tile([P, width], U32, name=name + "_w", align_bytes=64)
-            scales = keep.tile([P, width], U8, name=name + "_s", align_bytes=64)
+            codes = keep.tile([P, width], U32, name=name + "_w", align_bytes=MX_ALIGN)
+            scales = keep.tile([P, width], U8, name=name + "_s", align_bytes=MX_ALIGN)
             nc.vector.quantize_mx(out=codes[:].bitcast(FP8X4), scales=scales[:], in_=grouped[:])
             return codes, scales
 
-        def round_weight_block(raw, on_gpsimd):
-            grouped = work.tile([P, PACK * K_PASS], BF16, tag="wbf", bufs=3, align_bytes=64)
-            dst = grouped[:].rearrange("p (u e m j) -> p u m j e", u=2, e=2, j=PACK)
-            src = raw[:].rearrange("p j (m u e) -> p u m j e", u=2, e=2)
-            if on_gpsimd:
-                for u in range(2):
-                    nc.gpsimd.tensor_scalar(dst[:, u], src[:, u], 1.0, 0.0, ALU.mult, ALU.add)
-            else:
-                nc.vector.tensor_copy(out=dst, in_=src)
+        def round_weight_group(raw):
+            grouped = work.tile([P, PACK * K_PASS], BF16, tag="weights_bf16", bufs=3, align_bytes=MX_ALIGN)
+            nc.vector.tensor_copy(
+                out=grouped[:].rearrange("p (u e m j) -> p u m j e", u=2, e=2, j=PACK),
+                in_=raw[:].rearrange("p j (m u e) -> p u m j e", u=2, e=2),
+            )
             return grouped
 
-        def first_stage(lhs_w, lhs_s, rows, chunks, on_scalar):
-            for c in chunks:
-                bank = psum.tile([P, BANK], F32, tag="bank")
-                nc.tensor.matmul_mx(out=bank[:], lhsT=lhs_w, lhsT_scale=lhs_s, rhs=v_w[c][:].bitcast(FP8X4), rhs_scale=v_s[c][:], start=True, stop=True)
-                if on_scalar(c):
-                    nc.scalar.copy(out=rows[:, c * BANK : (c + 1) * BANK], in_=bank[:])
-                else:
-                    nc.vector.tensor_copy(out=rows[:, c * BANK : (c + 1) * BANK], in_=bank[:])
-
-        def gate_curved(curved, k):
-            b, t = divmod(k, PACK)
-            nc.vector.scalar_tensor_tensor(z[b][:, t, :], curved[:], lift_sb[:, k : k + 1], z[b][:, t, :], ALU.add, ALU.mult)
-
-        def interleave(planes, on_scalar=False):
-            grouped = work.tile([P, PACK * HALF], BF16, tag="abf", bufs=4, align_bytes=64)
-            copy = nc.scalar.copy if on_scalar else nc.vector.tensor_copy
+        def round_row_tiles(planes, copy):
+            grouped = work.tile([P, PACK * HALF], BF16, tag="rows_bf16", bufs=ROW_PASSES * HALVES, align_bytes=MX_ALIGN)
             copy(
                 out=grouped[:].rearrange("p (c i t) -> p c t i", i=4, t=PACK),
                 in_=planes.rearrange("p t (c i) -> p c t i", i=4),
             )
             return grouped
 
-        def g_stage(k, c, on_scalar):
+        def stationary(quantised, t):
+            codes, scales = quantised
+            return codes[:, P * t : P * (t + 1)].bitcast(FP8X4), scales[:, P * t : P * (t + 1)]
+
+        def first_stage(lhs_w, lhs_s, rows, c, copy):
+            bank = psum.tile([P, CHUNK], F32, tag="bank")
+            nc.tensor.matmul_mx(
+                out=bank[:], lhsT=lhs_w, lhsT_scale=lhs_s,
+                rhs=v_w[c][:].bitcast(FP8X4), rhs_scale=v_s[c][:], start=True, stop=True,
+            )
+            copy(out=rows[:, c * CHUNK : (c + 1) * CHUNK], in_=bank[:])
+
+
+        def g_stage(k, c, copy):
             b, t = divmod(k, PACK)
-            first_stage(w2_w[b][:, 2 * P * t : 2 * P * (t + 1)].bitcast(FP4X4), w2_s[b][:, P * t : P * (t + 1)], g_rows[k], (c,), lambda c: on_scalar)
+            first_stage(w2_w[b][:, 2 * P * t : 2 * P * (t + 1)].bitcast(FP4X4), w2_s[b][:, P * t : P * (t + 1)], g_rows[k], c, copy)
 
-        w1_q = []
-        curved = []
-        g_rows = []
+        def row_tile_window(tag):
+            return work.tile([P, S], F32, name="rows", tag=tag, bufs=ROW_TILES if tag == "rows" else 1)
+
+        g_tags = ["rows"] * (ROW_TILES - HALVES) + [f"g_then_a{half}" for half in reversed(range(HALVES))]
+
+        w1_q, c_rows, g_rows = [], [], []
         for k in range(G_BANKS_ON_SCALAR):
-            g = work.tile([P, S], F32, tag="rows", bufs=8)
-            g_rows.append(g)
-            g_stage(k, 0, True)
+            g_rows.append(row_tile_window(g_tags[k]))
+            g_stage(k, 0, nc.scalar.copy)
         for k in range(ROW_TILES):
-            last = k >= ROW_TILES - 2
             if k >= G_BANKS_ON_SCALAR:
-                g = work.tile([P, S], F32, tag=f"turn{ROW_TILES - 1 - k}" if last else "rows", bufs=1 if last else 8)
-                g_rows.append(g)
-                g_stage(k, 0, False)
-            g_stage(k, 1, False)
-            tile = work.tile([P, PAIRS], F32, tag="curved", bufs=8)
-            nc.scalar.activation(out=tile[:], in_=g_rows[k][:].indirect(pos2_sb[:]), func=ACT.Sigmoid, bias=thr_sb[:, k : k + 1])
-            curved.append(tile)
+                g_rows.append(row_tile_window(g_tags[k]))
+                g_stage(k, 0, nc.vector.tensor_copy)
+            g_stage(k, 1, nc.vector.tensor_copy)
+            c_tile = work.tile([P, PAIRS], F32, tag="c_rows", bufs=ROW_TILES)
+            nc.scalar.activation(out=c_tile[:], in_=g_rows[k][:].indirect(pos2_sb[:]), func=ACT.Sigmoid, bias=thr_sb[:, k : k + 1])
+            c_rows.append(c_tile)
             if k in W1_ROUND_AFTER:
-                w1_bf = round_weight_block(w1_raw[len(w1_q)], False)
+                w1_bf16 = round_weight_group(w1_raw[len(w1_q)])
             if k - 1 in W1_ROUND_AFTER:
-                w1_q.append(quantize(w1_bf, f"w1_q{len(w1_q)}"))
+                w1_q.append(quantize(w1_bf16, f"w1_q{len(w1_q)}"))
 
-        flat = {}
 
-        def look_flat(h, k, half):
+        a_rows, h_rows = {}, []
+
+        def look_into_h(k, half):
             b, t = divmod(k, PACK)
             if t == 0:
-                first = b == 0
-                flat[b, half] = work.tile([P, PACK, HALF], F32, name="flat", tag=f"turn{half}" if first else "flat", bufs=1 if first else 2)
+                tag, bufs = (f"g_then_a{half}", 1) if b == 0 else ("a_rows", HALVES)
+                a_rows[b, half] = work.tile([P, PACK, HALF], F32, name="a_rows", tag=tag, bufs=bufs)
+            offsets = pos1_sb[:, half * HALF // PER_COLUMN : (half + 1) * HALF // PER_COLUMN]
             nc.scalar.activation(
-                out=flat[b, half][:, t, :], in_=h[:].indirect(pos1_sb[:, 16 * half : 16 * (half + 1)]), func=ACT.Exp,
+                out=a_rows[b, half][:, t, :], in_=h_rows[k][:].indirect(offsets), func=ACT.Exp,
                 bias=shift_sb[:, k : k + 1], scale=temp_sb[:, k : k + 1],
             )
 
-        def finish_z(b, half, ts):
-            cols = slice(half * HALF, (half + 1) * HALF)
-            nc.vector.tensor_tensor(z[b][:, ts, cols], z[b][:, ts, cols], flat[b, half][:, ts, :], ALU.mult)
-
-        def h_stage(k, chunks, on_scalar):
-            b, t = divmod(k, PACK)
-            codes, scales = w1_q[b]
-            first_stage(codes[:, P * t : P * (t + 1)].bitcast(FP8X4), scales[:, P * t : P * (t + 1)], h_rows[k], chunks, lambda c: on_scalar)
-
-        h_rows = []
-        w3_q = {}
-        z_q = {}
         for k in range(ROW_TILES):
-            h = work.tile([P, S], F32, tag="rows", bufs=8)
-            h_rows.append(h)
-            for c in range(S // BANK):
-                h_stage(k, (c,), 2 * k + c >= H_BANKS_ON_VECTOR)
-            look_flat(h, k, 0)
-            if k < PACK:
-                look_flat(h, k, 1)
+            b, t = divmod(k, PACK)
+            h_rows.append(row_tile_window("rows"))
+            for c in range(CHUNKS):
+                copy = nc.vector.tensor_copy if CHUNKS * k + c < H_BANKS_ON_VECTOR else nc.scalar.copy
+                first_stage(*stationary(w1_q[b], t), h_rows[k], c, copy)
+            look_into_h(k, 0)
+            if b == 0:
+                look_into_h(k, 1)
         for k in range(PACK, ROW_TILES):
-            look_flat(h_rows[k], k, 1)
+            look_into_h(k, 1)
 
-        def finish_and_quantize_z(b, half):
-            for u in range(4):
-                finish_z(b, half, slice(u * 1, (u + 1) * 1))
-            z_q[b, half] = quantize(interleave(z[b][:, :, half * HALF : (half + 1) * HALF]), f"z_q{b}{half}")
 
-        w3_order = list(w3_raw)
-        for step in range(len(w3_order)):
-            gate_curved(curved[2 * step], 2 * step)
-            rounded = round_weight_block(w3_raw[w3_order[step]], False)
-            gate_curved(curved[2 * step + 1], 2 * step + 1)
-            w3_q[w3_order[step]] = quantize(rounded, f"w3_q{step}")
+        def times_c_plus_lift(k):
+            b, t = divmod(k, PACK)
+            nc.vector.scalar_tensor_tensor(z[b][:, t, :], c_rows[k][:], lift_sb[:, k : k + 1], z[b][:, t, :], ALU.add, ALU.mult)
+
+        w3_q = {}
+        for step, group in enumerate(w3_raw):
+            times_c_plus_lift(2 * step)
+            w3_bf16 = round_weight_group(w3_raw[group])
+            times_c_plus_lift(2 * step + 1)
+            w3_q[group] = quantize(w3_bf16, f"w3_q{step}")
+
+
+        z_q = {}
         for b in range(ROW_PASSES):
-            for half in range(2):
-                finish_and_quantize_z(b, half)
+            for half in range(HALVES):
+                cols = slice(half * HALF, (half + 1) * HALF)
+                for t in range(PACK):
+                    one = slice(t, t + 1)
+                    nc.vector.tensor_tensor(z[b][:, one, cols], z[b][:, one, cols], a_rows[b, half][:, one, :], ALU.mult)
+                z_q[b, half] = quantize(round_row_tiles(z[b][:, :, cols], nc.vector.tensor_copy), f"z_q{b}{half}")
+
 
         y = {}
-        for half in range(2):
+        for half in range(HALVES):
             for b in range(ROW_PASSES):
-                y[b, half] = work.tile([P, PACK, HALF], F32, name="y", tag="y", bufs=4)
+                y[b, half] = work.tile([P, PACK, HALF], F32, name="y", tag="y", bufs=ROW_PASSES * HALVES)
                 for u in range(2):
                     bank = psum.tile([P, 2, HALF], F32, tag="bank")
                     for a in range(ROW_PASSES):
+                        z_codes, z_scales = z_q[a, half]
                         for e in range(2):
-                            t = 2 * u + e
-                            codes, scales = w3_q[a, b]
+                            lhs_w, lhs_s = stationary(w3_q[a, b], 2 * u + e)
                             nc.tensor.matmul_mx(
-                                out=bank[:, e, :], lhsT=codes[:, P * t : P * (t + 1)].bitcast(FP8X4), lhsT_scale=scales[:, P * t : P * (t + 1)],
-                                rhs=z_q[a, half][0][:].bitcast(FP8X4), rhs_scale=z_q[a, half][1][:],
+                                out=bank[:, e, :], lhsT=lhs_w, lhsT_scale=lhs_s,
+                                rhs=z_codes[:].bitcast(FP8X4), rhs_scale=z_scales[:],
                                 start=(a == 0 and e == 0), stop=(a == ROW_PASSES - 1 and e == 1),
                             )
                     nc.scalar.activation(out=y[b, half][:, 2 * u : 2 * u + 2, :], in_=bank[:], func=ACT.Tanh)
 
+
         out_rows = out.rearrange("(n p) j -> p n j", p=P)
-        for half in range(2):
+        for half in range(HALVES):
             cols = slice(half * HALF, (half + 1) * HALF)
             y_q = []
             for b in range(ROW_PASSES):
                 for t in range(PACK):
                     k = PACK * b + t
-                    plane = y[b, half][:, t, :]
-                    nc.vector.scalar_tensor_tensor(plane, plane, gain_sb[:, k : k + 1], z[b][:, t, cols], ALU.mult, ALU.add)
-                y_q.append(quantize(interleave(y[b, half][:], 2 * half + b < 2), f"y_q{b}{half}"))
-            scores = work.tile([P, N // P, HALF], F32, tag="scores", bufs=2)
+                    y_tile = y[b, half][:, t, :]
+                    nc.vector.scalar_tensor_tensor(y_tile, y_tile, gain_sb[:, k : k + 1], z[b][:, t, cols], ALU.mult, ALU.add)
+                copy = nc.scalar.copy if half == 0 else nc.vector.tensor_copy
+                y_q.append(quantize(round_row_tiles(y[b, half][:], copy), f"y_q{b}{half}"))
+            scores = work.tile([P, N // P, HALF], F32, tag="scores", bufs=HALVES)
             for n in range(N // P):
                 bank = psum.tile([P, HALF], F32, tag="bank")
                 n_cols = slice(P * n, P * (n + 1))
                 for a in range(ROW_PASSES):
+                    y_codes, y_scales = y_q[a]
                     nc.tensor.matmul_mx(
                         out=bank[:], lhsT=w4_w[:, a, n_cols].bitcast(FP8X4), lhsT_scale=w4_s[:, a, n_cols],
-                        rhs=y_q[a][0][:].bitcast(FP8X4), rhs_scale=y_q[a][1][:],
+                        rhs=y_codes[:].bitcast(FP8X4), rhs_scale=y_scales[:],
                         start=(a == 0), stop=(a == ROW_PASSES - 1),
                     )
-                if half == 1 and n == 1:
-                    nc.vector.tensor_copy(out=scores[:, n, :], in_=bank[:])
-                else:
-                    nc.scalar.copy(out=scores[:, n, :], in_=bank[:])
+                copy = nc.vector.tensor_copy if half == HALVES - 1 and n == 1 else nc.scalar.copy
+                copy(out=scores[:, n, :], in_=bank[:])
             nc.sync.dma_start(out=out_rows[:, :, cols], in_=scores[:])

from contextlib import ExitStack

import concourse.mybir as mybir

K, H, N, T, S, PAIRS = 512, 1024, 384, 2048, 1024, 512
FLOPS = 2 * (2 * K * H * S + H * H * PAIRS + H * N * PAIRS)

F32 = mybir.dt.float32
BF16 = mybir.dt.bfloat16
I32 = mybir.dt.int32
U32 = mybir.dt.uint32
U16 = mybir.dt.uint16
U8 = mybir.dt.uint8
FP8X4 = mybir.dt.float8_e4m3fn_x4
FP4X4 = mybir.dt.float4_e2m1fn_x4
ACT = mybir.ActivationFunctionType
ALU = mybir.AluOpType

P = 128
PACK = 4
K_PASS = P * PACK
CHUNK = 512
CHUNKS = S // CHUNK
PER_COLUMN = 16
ROW_PASSES = H // K_PASS
ROW_TILES = H // P
HALVES = 2
HALF = PAIRS // HALVES
PSUM_BANKS = 8
MX_ALIGN = 64

G_BANKS_ON_SCALAR = 5
H_BANKS_ON_VECTOR = 5
W1_ROUND_AFTER = (2, 5)


def tile_list_suction_seal_scores_kernel(
    tc, tab_words, tab_scales, offs, pos1, pos2, w1, w2_words, w2_scales,
    temp, shift, thr, lift, mat, w3, gain, w4_words, w4_scales, out,
):
    nc = tc.nc
    with ExitStack() as ctx:
        lists = ctx.enter_context(tc.tile_pool(name="lists", bufs=1))
        keep = ctx.enter_context(tc.tile_pool(name="keep", bufs=1))
        work = ctx.enter_context(tc.tile_pool(name="work", bufs=1))
        psum = ctx.enter_context(tc.psum_pool(name="psum", bufs=PSUM_BANKS))


        def load_scale_rows(queue, scale_tile, rows):
            for quadrant in range(4):
                queue.dma_start(
                    out=scale_tile[32 * quadrant : 32 * quadrant + 4].bitcast(I32),
                    in_=rows[4 * quadrant : 4 * quadrant + 4].bitcast(I32),
                )

        def load_row_vector(vec, name):
            columns = keep.tile([P, ROW_TILES], F32, name=name)
            nc.sync.dma_start(
                out=columns[:].rearrange("p (b t) -> p b t", t=PACK),
                in_=vec.rearrange("(b p t) -> p b t", p=P, t=PACK),
            )
            return columns

        def load_weight_group(w, a, b, name):
            raw = keep.tile([P, PACK, K_PASS], F32, name=name)
            rows = w[a * K_PASS : (a + 1) * K_PASS, b * K_PASS : (b + 1) * K_PASS]
            nc.sync.dma_start(out=raw[:], in_=rows.rearrange("(p j) c -> p j c", j=PACK))
            return raw

        tab_s = work.tile([P, T], U8, tag="tab_s_then_words", bufs=1, align_bytes=MX_ALIGN)
        w2_s_raw = keep.tile([P, H], U8, align_bytes=MX_ALIGN)
        w4_s = keep.tile([P, ROW_PASSES, N], U8, align_bytes=MX_ALIGN)
        nc.gpsimd.memset(tab_s[:].bitcast(I32), 0)
        nc.vector.memset(w2_s_raw[:].bitcast(I32), 0)

        offs_sb = lists.tile([P, S // PER_COLUMN], U16)
        nc.sync.dma_start(offs_sb[:], offs)
        load_scale_rows(nc.scalar, tab_s, tab_scales[0])
        tab_w = keep.tile([P, T], U32, align_bytes=MX_ALIGN)
        nc.sync.dma_start(out=tab_w[:].bitcast(I32), in_=tab_words[0].rearrange("p t i -> p (t i)").bitcast(I32))
        w2_w_raw = keep.tile([P, 2 * H], U8, align_bytes=MX_ALIGN)
        nc.sync.dma_start(out=w2_w_raw[:].bitcast(I32), in_=w2_words[0].bitcast(I32))
        load_scale_rows(nc.sync, w2_s_raw, w2_scales[0])
        nc.vector.memset(w4_s[:].rearrange("p a n -> p (a n)").bitcast(I32), 0)

        w1_raw = [load_weight_group(w1, 0, 0, "w1_raw0")]
        pos2_sb = lists.tile([P, PAIRS // PER_COLUMN], U16)
        nc.sync.dma_start(pos2_sb[:], pos2)
        thr_sb = load_row_vector(thr, "thr_sb")
        w1_raw.append(load_weight_group(w1, 0, 1, "w1_raw1"))
        pos1_sb = lists.tile([P, PAIRS // PER_COLUMN], U16)
        nc.sync.dma_start(pos1_sb[:], pos1)
        temp_sb = load_row_vector(temp, "temp_sb")
        shift_sb = load_row_vector(shift, "shift_sb")
        lift_sb = load_row_vector(lift, "lift_sb")
        z = []
        for b in range(ROW_PASSES):
            mat_sb = keep.tile([P, PACK, PAIRS], F32, name=f"z{b}")
            nc.sync.dma_start(out=mat_sb[:], in_=mat[b * K_PASS : (b + 1) * K_PASS].rearrange("(p t) c -> p t c", t=PACK))
            z.append(mat_sb)
        gain_sb = load_row_vector(gain, "gain_sb")
        w3_raw = {
            (a, b): load_weight_group(w3, a, b, f"w3_raw{a}{b}") for b in range(ROW_PASSES) for a in range(ROW_PASSES)
        }
        w4_w = keep.tile([P, ROW_PASSES, N], U32, align_bytes=MX_ALIGN)
        nc.sync.dma_start(out=w4_w[:].bitcast(I32), in_=w4_words.rearrange("a p n i -> p a (n i)").bitcast(I32))
        load_scale_rows(nc.sync, w4_s, w4_scales.rearrange("a r n -> r a n"))


        chunk_offsets = [offs_sb[:, c * CHUNK // PER_COLUMN : (c + 1) * CHUNK // PER_COLUMN] for c in range(CHUNKS)]
        v_w, v_s = [], []
        for c in range(CHUNKS):
            picked_s = keep.tile([P, CHUNK], U8, name=f"v_s{c}", align_bytes=MX_ALIGN)
            nc.vector.tensor_copy(picked_s[:], tab_s[:].indirect(chunk_offsets[c]))
            v_s.append(picked_s)
        for c in range(CHUNKS):
            picked_w = work.tile([P, CHUNK], U32, tag="tab_s_then_words" if c else "v_w0", bufs=1, align_bytes=MX_ALIGN)
            nc.vector.tensor_copy(picked_w[:], tab_w[:].indirect(chunk_offsets[c]))
            v_w.append(picked_w)


        w2_w, w2_s = [], []
        for b in range(ROW_PASSES):
            dealt_w = keep.tile([P, 2 * K_PASS], U8, name=f"w2_w{b}", align_bytes=MX_ALIGN)
            nc.scalar.copy(
                out=dealt_w[:].bitcast(U16).rearrange("p (t m) -> p t m", t=PACK),
                in_=w2_w_raw[:, 2 * K_PASS * b : 2 * K_PASS * (b + 1)].bitcast(U16).rearrange("p (m t) -> p t m", t=PACK),
            )
            dealt_s = keep.tile([P, K_PASS], U8, name=f"w2_s{b}", align_bytes=MX_ALIGN)
            for t in range(PACK):
                nc.gpsimd.tensor_copy(
                    out=dealt_s[:, P * t : P * (t + 1)],
                    in_=w2_s_raw[:, K_PASS * b + t : K_PASS * (b + 1) : PACK],
                )
            w2_w.append(dealt_w)
            w2_s.append(dealt_s)


        def quantize(grouped, name):
            width = grouped.shape[1] // PACK
            codes = keep.tile([P, width], U32, name=name + "_w", align_bytes=MX_ALIGN)
            scales = keep.tile([P, width], U8, name=name + "_s", align_bytes=MX_ALIGN)
            nc.vector.quantize_mx(out=codes[:].bitcast(FP8X4), scales=scales[:], in_=grouped[:])
            return codes, scales

        def round_weight_group(raw):
            grouped = work.tile([P, PACK * K_PASS], BF16, tag="weights_bf16", bufs=3, align_bytes=MX_ALIGN)
            nc.vector.tensor_copy(
                out=grouped[:].rearrange("p (u e m j) -> p u m j e", u=2, e=2, j=PACK),
                in_=raw[:].rearrange("p j (m u e) -> p u m j e", u=2, e=2),
            )
            return grouped

        def round_row_tiles(planes, copy):
            grouped = work.tile([P, PACK * HALF], BF16, tag="rows_bf16", bufs=ROW_PASSES * HALVES, align_bytes=MX_ALIGN)
            copy(
                out=grouped[:].rearrange("p (c i t) -> p c t i", i=4, t=PACK),
                in_=planes.rearrange("p t (c i) -> p c t i", i=4),
            )
            return grouped

        def stationary(quantised, t):
            codes, scales = quantised
            return codes[:, P * t : P * (t + 1)].bitcast(FP8X4), scales[:, P * t : P * (t + 1)]

        def first_stage(lhs_w, lhs_s, rows, c, copy):
            bank = psum.tile([P, CHUNK], F32, tag="bank")
            nc.tensor.matmul_mx(
                out=bank[:], lhsT=lhs_w, lhsT_scale=lhs_s,
                rhs=v_w[c][:].bitcast(FP8X4), rhs_scale=v_s[c][:], start=True, stop=True,
            )
            copy(out=rows[:, c * CHUNK : (c + 1) * CHUNK], in_=bank[:])


        def g_stage(k, c, copy):
            b, t = divmod(k, PACK)
            first_stage(w2_w[b][:, 2 * P * t : 2 * P * (t + 1)].bitcast(FP4X4), w2_s[b][:, P * t : P * (t + 1)], g_rows[k], c, copy)

        def row_tile_window(tag):
            return work.tile([P, S], F32, name="rows", tag=tag, bufs=ROW_TILES if tag == "rows" else 1)

        g_tags = ["rows"] * (ROW_TILES - HALVES) + [f"g_then_a{half}" for half in reversed(range(HALVES))]

        w1_q, c_rows, g_rows = [], [], []
        for k in range(G_BANKS_ON_SCALAR):
            g_rows.append(row_tile_window(g_tags[k]))
            g_stage(k, 0, nc.scalar.copy)
        for k in range(ROW_TILES):
            if k >= G_BANKS_ON_SCALAR:
                g_rows.append(row_tile_window(g_tags[k]))
                g_stage(k, 0, nc.vector.tensor_copy)
            g_stage(k, 1, nc.vector.tensor_copy)
            c_tile = work.tile([P, PAIRS], F32, tag="c_rows", bufs=ROW_TILES)
            nc.scalar.activation(out=c_tile[:], in_=g_rows[k][:].indirect(pos2_sb[:]), func=ACT.Sigmoid, bias=thr_sb[:, k : k + 1])
            c_rows.append(c_tile)
            if k in W1_ROUND_AFTER:
                w1_bf16 = round_weight_group(w1_raw[len(w1_q)])
            if k - 1 in W1_ROUND_AFTER:
                w1_q.append(quantize(w1_bf16, f"w1_q{len(w1_q)}"))


        a_rows, h_rows = {}, []

        def look_into_h(k, half):
            b, t = divmod(k, PACK)
            if t == 0:
                tag, bufs = (f"g_then_a{half}", 1) if b == 0 else ("a_rows", HALVES)
                a_rows[b, half] = work.tile([P, PACK, HALF], F32, name="a_rows", tag=tag, bufs=bufs)
            offsets = pos1_sb[:, half * HALF // PER_COLUMN : (half + 1) * HALF // PER_COLUMN]
            nc.scalar.activation(
                out=a_rows[b, half][:, t, :], in_=h_rows[k][:].indirect(offsets), func=ACT.Exp,
                bias=shift_sb[:, k : k + 1], scale=temp_sb[:, k : k + 1],
            )

        for k in range(ROW_TILES):
            b, t = divmod(k, PACK)
            h_rows.append(row_tile_window("rows"))
            for c in range(CHUNKS):
                copy = nc.vector.tensor_copy if CHUNKS * k + c < H_BANKS_ON_VECTOR else nc.scalar.copy
                first_stage(*stationary(w1_q[b], t), h_rows[k], c, copy)
            look_into_h(k, 0)
            if b == 0:
                look_into_h(k, 1)
        for k in range(PACK, ROW_TILES):
            look_into_h(k, 1)


        def times_c_plus_lift(k):
            b, t = divmod(k, PACK)
            nc.vector.scalar_tensor_tensor(z[b][:, t, :], c_rows[k][:], lift_sb[:, k : k + 1], z[b][:, t, :], ALU.add, ALU.mult)

        w3_q = {}
        for step, group in enumerate(w3_raw):
            times_c_plus_lift(2 * step)
            w3_bf16 = round_weight_group(w3_raw[group])
            times_c_plus_lift(2 * step + 1)
            w3_q[group] = quantize(w3_bf16, f"w3_q{step}")


        z_q = {}
        for b in range(ROW_PASSES):
            for half in range(HALVES):
                cols = slice(half * HALF, (half + 1) * HALF)
                for t in range(PACK):
                    one = slice(t, t + 1)
                    nc.vector.tensor_tensor(z[b][:, one, cols], z[b][:, one, cols], a_rows[b, half][:, one, :], ALU.mult)
                z_q[b, half] = quantize(round_row_tiles(z[b][:, :, cols], nc.vector.tensor_copy), f"z_q{b}{half}")


        y = {}
        for half in range(HALVES):
            for b in range(ROW_PASSES):
                y[b, half] = work.tile([P, PACK, HALF], F32, name="y", tag="y", bufs=ROW_PASSES * HALVES)
                for u in range(2):
                    bank = psum.tile([P, 2, HALF], F32, tag="bank")
                    for a in range(ROW_PASSES):
                        z_codes, z_scales = z_q[a, half]
                        for e in range(2):
                            lhs_w, lhs_s = stationary(w3_q[a, b], 2 * u + e)
                            nc.tensor.matmul_mx(
                                out=bank[:, e, :], lhsT=lhs_w, lhsT_scale=lhs_s,
                                rhs=z_codes[:].bitcast(FP8X4), rhs_scale=z_scales[:],
                                start=(a == 0 and e == 0), stop=(a == ROW_PASSES - 1 and e == 1),
                            )
                    nc.scalar.activation(out=y[b, half][:, 2 * u : 2 * u + 2, :], in_=bank[:], func=ACT.Tanh)


        out_rows = out.rearrange("(n p) j -> p n j", p=P)
        for half in range(HALVES):
            cols = slice(half * HALF, (half + 1) * HALF)
            y_q = []
            for b in range(ROW_PASSES):
                for t in range(PACK):
                    k = PACK * b + t
                    y_tile = y[b, half][:, t, :]
                    nc.vector.scalar_tensor_tensor(y_tile, y_tile, gain_sb[:, k : k + 1], z[b][:, t, cols], ALU.mult, ALU.add)
                copy = nc.scalar.copy if half == 0 else nc.vector.tensor_copy
                y_q.append(quantize(round_row_tiles(y[b, half][:], copy), f"y_q{b}{half}"))
            scores = work.tile([P, N // P, HALF], F32, tag="scores", bufs=HALVES)
            for n in range(N // P):
                bank = psum.tile([P, HALF], F32, tag="bank")
                n_cols = slice(P * n, P * (n + 1))
                for a in range(ROW_PASSES):
                    y_codes, y_scales = y_q[a]
                    nc.tensor.matmul_mx(
                        out=bank[:], lhsT=w4_w[:, a, n_cols].bitcast(FP8X4), lhsT_scale=w4_s[:, a, n_cols],
                        rhs=y_codes[:].bitcast(FP8X4), rhs_scale=y_scales[:],
                        start=(a == 0), stop=(a == ROW_PASSES - 1),
                    )
                copy = nc.vector.tensor_copy if half == HALVES - 1 and n == 1 else nc.scalar.copy
                copy(out=scores[:, n, :], in_=bank[:])
            nc.sync.dma_start(out=out_rows[:, :, cols], in_=scores[:])
